import numpy as np
import ml_dtypes


def mxq(x, axis, fmt="e4m3"):
    dtype, down = {"e4m3": (ml_dtypes.float8_e4m3fn, 7), "e5m2": (ml_dtypes.float8_e5m2, 14)}[fmt]
    v = np.moveaxis(np.asarray(x, np.float32).astype(ml_dtypes.bfloat16).astype(np.float64), axis, -1)
    blocks = v.reshape(v.shape[:-1] + (-1, 32))
    amax = np.abs(blocks).max(-1, keepdims=True)
    byte = np.maximum(np.where(amax > 0, np.frexp(amax)[1] - 1 + 127, 0) - down, 1)
    scale = np.exp2(byte - 127.0)
    codes = (blocks / scale).astype(np.float32).astype(dtype).astype(np.float64)
    return np.moveaxis((codes * scale).reshape(v.shape), -1, axis)


WIDE = False


def mx_kscale(k):
    if not WIDE:
        return np.ones(k)
    levels = np.array([10, -10, 5, -5, 0])
    if k % 512:
        return np.exp2(np.random.permutation(np.resize(levels, k // 32))).repeat(32)
    a = np.empty((k // 512, 16))
    for p in range(k // 512):
        a[p, :8] = np.random.permutation(np.resize(levels, 8))
        for g in range(8):
            far = levels[np.abs(levels - a[p, g]) >= 10]
            a[p, g + 8] = far[np.random.randint(len(far))]
    return np.exp2(a.ravel()).repeat(32)


def f64(x):
    return np.asarray(x).astype(np.float64)


def striped8(idx):
    return np.asarray(idx).reshape(8, -1, 16).transpose(0, 2, 1).reshape(128, -1).astype(np.uint16)


def unstriped8(offs):
    return offs.reshape(8, 16, -1).transpose(0, 2, 1).reshape(8, -1).astype(np.int64)


def pick8(x, idx, run):
    r = np.arange(len(x))
    return x[r[:, None], idx[r % (8 * run) // run]]


E2M1 = np.array([0.0, 0.5, 1.0, 1.5, 2.0, 3.0, 4.0, 6.0, -0.0, -0.5, -1.0, -1.5, -2.0, -3.0, -4.0, -6.0])


def pack_weight(w, fmt):
    k, n = w.shape
    w = f64(np.asarray(w, np.float32).astype(ml_dtypes.bfloat16)).reshape(k // 32, 32, n)
    amax = np.abs(w).max(1)
    if fmt == "e4m3":
        byte = np.frexp(amax)[1] - 1 + 127 - 7
    else:
        mant, ex = np.frexp(amax / 6.0)
        byte = np.where(mant > 0.5, ex, ex - 1) + 127
    byte = np.clip(np.where(amax > 0, byte, 1), 1, 254)
    scaled = (w * np.exp2(127.0 - byte)[:, None, :]).reshape(k, n).astype(np.float32)
    by_word = np.ascontiguousarray(scaled.reshape(k // 512, 128, 4, n).transpose(0, 1, 3, 2))
    if fmt == "e4m3":
        words = by_word.astype(ml_dtypes.float8_e4m3fn).view(np.uint8)
    else:
        c = by_word.astype(ml_dtypes.float4_e2m1fn).view(np.uint8) & 0xF
        words = (c[..., 0::2] | (c[..., 1::2] << 4)).reshape(k // 512, 128, 2 * n)
    return np.ascontiguousarray(words), np.ascontiguousarray(byte.astype(np.uint8).reshape(k // 512, 16, n))


def unpack_weight(words, scales, fmt):
    g, _, n = scales.shape
    words = np.ascontiguousarray(words).reshape(g, 128, n, -1)
    if fmt == "e4m3":
        vals = words.view(ml_dtypes.float8_e4m3fn).astype(np.float64)
    else:
        nib = np.empty((g, 128, n, 4), np.uint8)
        nib[..., 0::2] = words & 0xF
        nib[..., 1::2] = words >> 4
        vals = E2M1[nib]
    vals = vals * np.repeat(np.exp2(scales.astype(np.float64) - 127.0), 8, axis=1)[..., None]
    return vals.transpose(0, 1, 3, 2).reshape(g * 512, n)


D, T, U, X, S, I, Q = 512, 1024, 1024, 1024, 1024, 512, 128


def setup_inputs():
    n = np.random.standard_normal
    idx = np.stack([np.random.permutation(T)[:I] for _ in range(8)])
    idx2 = np.stack([np.random.permutation(U)[:I] for _ in range(8)])
    idx3 = np.stack([np.random.permutation(U)[:I] for _ in range(8)])
    idx4 = np.stack([np.random.permutation(X)[:I] for _ in range(8)])
    idx5 = np.stack([np.random.permutation(S)[:I] for _ in range(8)])
    idx6 = np.stack([np.random.permutation(S)[:I] for _ in range(8)])
    fd = mx_kscale(D)
    keysp = pack_weight(n((D, T)) / fd[:, None], "e4m3")
    notesp = pack_weight(n((D, U)) / fd[:, None], "e2m1")
    usersp = pack_weight(n((D, X)) / fd[:, None], "e4m3")
    shelvesp = pack_weight(n((D, S)) / fd[:, None], "e2m1")
    return {
        "query": (n((D, Q)) * 1.0 / np.sqrt(D) * fd[:, None]).astype(np.float32),
        "keys_words": keysp[0],
        "keys_scales": keysp[1],
        "notes_words": notesp[0],
        "notes_scales": notesp[1],
        "users_words": usersp[0],
        "users_scales": usersp[1],
        "shelves_words": shelvesp[0],
        "shelves_scales": shelvesp[1],
        "offs": striped8(idx),
        "offs2": striped8(idx2),
        "offs3": striped8(idx3),
        "offs4": striped8(idx4),
        "offs5": striped8(idx5),
        "offs6": striped8(idx6),
    }


def reference(query, keys_words, keys_scales, notes_words, notes_scales, users_words, users_scales, shelves_words, shelves_scales, offs, offs2, offs3, offs4, offs5, offs6):
    idx = unstriped8(offs)
    idx2 = unstriped8(offs2)
    idx3 = unstriped8(offs3)
    idx4 = unstriped8(offs4)
    idx5 = unstriped8(offs5)
    idx6 = unstriped8(offs6)
    keysu = unpack_weight(keys_words, keys_scales, "e4m3")
    notesu = unpack_weight(notes_words, notes_scales, "e2m1")
    usersu = unpack_weight(users_words, users_scales, "e4m3")
    shelvesu = unpack_weight(shelves_words, shelves_scales, "e2m1")
    queryq = mxq(f64(query), 0, "e4m3")
    a = queryq.T @ keysu
    b = queryq.T @ notesu
    c0 = queryq.T @ usersu
    d0 = queryq.T @ shelvesu
    f1 = np.zeros((Q, U))
    f1[np.arange(Q)[:, None], idx2[np.arange(Q) % 128 // 16]] = pick8(a, idx, 16)
    bb = b + f1
    w = np.maximum(pick8(bb, idx3, 16), pick8(c0, idx4, 16))
    f2 = np.zeros((Q, S))
    f2[np.arange(Q)[:, None], idx5[np.arange(Q) % 128 // 16]] = w
    dd = d0 - f2
    y = pick8(dd, idx6, 16) + pick8(c0, idx4, 16)
    return y

@@ -1,0 +1,156 @@
+from contextlib import ExitStack
+
+import concourse.mybir as mybir
+
+FLOPS = 536870912
+
+F32 = mybir.dt.float32
+BF16 = mybir.dt.bfloat16
+I32 = mybir.dt.int32
+U32 = mybir.dt.uint32
+U16 = mybir.dt.uint16
+U8 = mybir.dt.uint8
+FP8X4 = mybir.dt.float8_e4m3fn_x4
+FP4X4 = mybir.dt.float4_e2m1fn_x4
+ADD = mybir.AluOpType.add
+SUB = mybir.AluOpType.subtract
+MAX = mybir.AluOpType.max
+COPY = mybir.ActivationFunctionType.Copy
+
+P = 128
+PACK = 4
+Q = 128
+POOL = 1024
+SLOTS = 512
+HALF = SLOTS // 2
+LIST_COLS = SLOTS // 16
+BANK = 512
+QUARTER = 256
+
+
+def tile_attend_estuary_four_kernel(tc, query, keys_words, keys_scales, notes_words, notes_scales,
+                                     users_words, users_scales, shelves_words, shelves_scales,
+                                     offs, offs2, offs3, offs4, offs5, offs6, out):
+    nc = tc.nc
+    with ExitStack() as ctx:
+        sb = ctx.enter_context(tc.tile_pool(name="sb", bufs=1))
+        ps = ctx.enter_context(tc.psum_pool(name="ps", bufs=1))
+
+        def load_list(src, name):
+            tile = sb.tile([P, LIST_COLS], U16, name=name)
+            nc.sync.dma_start(tile[:], src)
+            return tile
+
+        def half_of(offsets, h):
+            return offsets[:, h * (LIST_COLS // 2):(h + 1) * (LIST_COLS // 2)]
+
+        def zeroed_plane(name):
+            plane = sb.tile([P, POOL], U8, name=name, align_bytes=64)
+            nc.vector.memset(plane[:].bitcast(I32), 0)
+            return plane
+
+        def load_plane(plane, src):
+            rows = src[0].bitcast(I32)
+            for quad in range(4):
+                nc.sync.dma_start(plane[32 * quad:32 * quad + 4, :].bitcast(I32), rows[4 * quad:4 * quad + 4, :])
+
+        def load_words(src, c0, c1, name):
+            tile = sb.tile([P, c1 - c0], U8, name=name, align_bytes=64)
+            nc.sync.dma_start(tile[:].bitcast(I32), src[:, c0:c1].bitcast(I32))
+            return tile
+
+        keys_plane = zeroed_plane("keys_plane")
+        users_plane = zeroed_plane("users_plane")
+        notes_plane = zeroed_plane("notes_plane")
+        shelves_plane = zeroed_plane("shelves_plane")
+        f1 = sb.tile([P, POOL], F32, name="f1")
+        nc.vector.memset(f1[:], 0.0)
+        f2 = sb.tile([P, POOL], F32, name="f2")
+        nc.vector.memset(f2[:], 0.0)
+
+        q_raw = sb.tile([P, PACK, Q], F32, name="q_raw")
+        nc.sync.dma_start(q_raw[:], query.rearrange("(p j) q -> p j q", j=PACK))
+        keys_bytes = keys_words[0].rearrange("p n t -> p (n t)")
+        keys_w = [load_words(keys_bytes, h * BANK * 4, (h + 1) * BANK * 4, "keys_w%d" % h) for h in range(2)]
+        l1 = load_list(offs, "l1")
+        load_plane(keys_plane, keys_scales)
+        l2 = load_list(offs2, "l2")
+        users_w = load_words(users_words[0].rearrange("p n t -> p (n t)"), 0, POOL * 4, "users_w")
+        load_plane(users_plane, users_scales)
+        l4 = load_list(offs4, "l4")
+        notes_w = load_words(notes_words[0], 0, POOL * 2, "notes_w")
+        load_plane(notes_plane, notes_scales)
+        l3 = load_list(offs3, "l3")
+        l5 = load_list(offs5, "l5")
+        shelves_w = load_words(shelves_words[0], 0, POOL * 2, "shelves_w")
+        load_plane(shelves_plane, shelves_scales)
+        l6 = load_list(offs6, "l6")
+
+        q_bf = sb.tile([P, Q, PACK], BF16, name="q_bf", align_bytes=64)
+        nc.vector.tensor_copy(q_bf[:], q_raw[:].rearrange("p j q -> p q j"))
+        q_codes = sb.tile([P, Q], U32, name="q_codes", align_bytes=64)
+        q_plane = sb.tile([P, Q], U8, name="q_plane", align_bytes=64)
+        nc.vector.quantize_mx(out=q_codes[:].bitcast(FP8X4), scales=q_plane[:],
+                              in_=q_bf[:].rearrange("p q j -> p (q j)"))
+
+        def scores(words, plane, width, tag):
+            bank = ps.tile([P, width], F32, name=tag, tag=tag)
+            nc.tensor.matmul_mx(out=bank[:], lhsT=q_codes[:].bitcast(FP8X4), lhsT_scale=q_plane[:],
+                                rhs=words, rhs_scale=plane, start=True, stop=True)
+            return bank
+
+        a_sb = sb.tile([P, POOL], F32, name="a_sb")
+        for j in range(POOL // QUARTER):
+            h, r = divmod(j, 2)
+            bank = scores(keys_w[h][:, r * QUARTER * 4:(r + 1) * QUARTER * 4].bitcast(FP8X4),
+                          keys_plane[:, j * QUARTER:(j + 1) * QUARTER], QUARTER, "bank_a%d" % j)
+            cols = slice(j * QUARTER, (j + 1) * QUARTER)
+            if j % 2 == 0:
+                nc.scalar.copy(a_sb[:, cols], bank[:])
+            else:
+                nc.vector.tensor_copy(a_sb[:, cols], bank[:])
+
+        for h in range(2):
+            ga = sb.tile([P, HALF], F32, name="ga%d" % h)
+            nc.scalar.activation(ga[:], a_sb[:].indirect(half_of(l1, h)), COPY)
+            nc.vector.tensor_copy(f1[:].indirect(half_of(l2, h)), ga[:])
+
+        c_sb = sb.tile([P, POOL], F32, name="c_sb")
+        for h in range(2):
+            bank = scores(users_w[:, h * BANK * 4:(h + 1) * BANK * 4].bitcast(FP8X4),
+                          users_plane[:, h * BANK:(h + 1) * BANK], BANK, "bank_a%d" % (2 + h))
+            nc.scalar.copy(c_sb[:, h * BANK:(h + 1) * BANK], bank[:])
+        cg = sb.tile([P, SLOTS], F32, name="cg")
+        nc.scalar.activation(cg[:], c_sb[:].indirect(l4[:]), COPY)
+
+        bb = sb.tile([P, POOL], F32, name="bb")
+        for h in range(2):
+            cols = slice(h * BANK, (h + 1) * BANK)
+            bank = scores(notes_w[:, h * BANK * 2:(h + 1) * BANK * 2].bitcast(FP4X4),
+                          notes_plane[:, cols], BANK, "bank_b%d" % h)
+            nc.vector.tensor_tensor(bb[:, cols], bank[:], f1[:, cols], ADD)
+
+        gb = [sb.tile([P, HALF], F32, name="gb%d" % h) for h in range(2)]
+        nc.scalar.activation(gb[0][:], bb[:].indirect(half_of(l3, 0)), COPY)
+        nc.vector.tensor_copy(gb[1][:], bb[:].indirect(half_of(l3, 1)))
+        w = [sb.tile([P, HALF], F32, name="w%d" % h) for h in range(2)]
+        for h in range(2):
+            nc.vector.tensor_tensor(w[h][:], gb[h][:], cg[:, h * HALF:(h + 1) * HALF], MAX)
+        for h in range(2):
+            nc.vector.tensor_copy(f2[:].indirect(half_of(l5, h)), w[h][:])
+
+        dd = sb.tile([P, POOL], F32, name="dd")
+        for h in range(2):
+            cols = slice(h * BANK, (h + 1) * BANK)
+            bank = scores(shelves_w[:, h * BANK * 2:(h + 1) * BANK * 2].bitcast(FP4X4),
+                          shelves_plane[:, cols], BANK, "bank_d%d" % h)
+            nc.vector.tensor_tensor(dd[:, cols], bank[:], f2[:, cols], SUB)
+
+        y0 = sb.tile([P, HALF], F32, name="y0")
+        nc.vector.tensor_tensor(y0[:], dd[:].indirect(half_of(l6, 0)), cg[:, 0:HALF], ADD)
+        nc.sync.dma_start(out[:, 0:HALF], y0[:])
+        gd = sb.tile([P, HALF], F32, name="gd")
+        nc.scalar.activation(gd[:], dd[:].indirect(half_of(l6, 1)), COPY)
+        y1 = sb.tile([P, HALF], F32, name="y1")
+        nc.vector.tensor_tensor(y1[:], gd[:], cg[:, HALF:SLOTS], ADD)
+        nc.sync.dma_start(out[:, HALF:SLOTS], y1[:])

@@ -26,6 +26,7 @@ HALF = SLOTS // 2
 LIST_COLS = SLOTS // 16
 BANK = 512
 QUARTER = 256
+Q_SCALAR = 40
 
 
 def tile_attend_estuary_four_kernel(tc, query, keys_words, keys_scales, notes_words, notes_scales,
@@ -44,9 +45,9 @@ def tile_attend_estuary_four_kernel(tc, query, keys_words, keys_scales, notes_wo
         def half_of(offsets, h):
             return offsets[:, h * (LIST_COLS // 2):(h + 1) * (LIST_COLS // 2)]
 
-        def zeroed_plane(name):
+        def zeroed_plane(name, engine):
             plane = sb.tile([P, POOL], U8, name=name, align_bytes=64)
-            nc.vector.memset(plane[:].bitcast(I32), 0)
+            engine.memset(plane[:].bitcast(I32), 0)
             return plane
 
         def load_plane(plane, src):
@@ -59,21 +60,23 @@ def tile_attend_estuary_four_kernel(tc, query, keys_words, keys_scales, notes_wo
             nc.sync.dma_start(tile[:].bitcast(I32), src[:, c0:c1].bitcast(I32))
             return tile
 
-        keys_plane = zeroed_plane("keys_plane")
-        users_plane = zeroed_plane("users_plane")
-        notes_plane = zeroed_plane("notes_plane")
-        shelves_plane = zeroed_plane("shelves_plane")
+        keys_plane = sb.tile([P, POOL], U8, name="keys_plane", align_bytes=64)
         f1 = sb.tile([P, POOL], F32, name="f1")
         nc.vector.memset(f1[:], 0.0)
-        f2 = sb.tile([P, POOL], F32, name="f2")
-        nc.vector.memset(f2[:], 0.0)
+        users_plane = zeroed_plane("users_plane", nc.vector)
+        notes_plane = zeroed_plane("notes_plane", nc.vector)
+        shelves_plane = zeroed_plane("shelves_plane", nc.vector)
 
         q_raw = sb.tile([P, PACK, Q], F32, name="q_raw")
         nc.sync.dma_start(q_raw[:], query.rearrange("(p j) q -> p j q", j=PACK))
+        key_rows = keys_scales[0].bitcast(I32)
+        for quad in range(4):
+            nc.sync.dma_start(keys_plane[32 * quad:32 * quad + 32, :].bitcast(I32),
+                              key_rows[4 * quad:4 * quad + 4, :].unsqueeze(0).to_broadcast([8, 4, POOL // 4]))
         keys_bytes = keys_words[0].rearrange("p n t -> p (n t)")
-        keys_w = [load_words(keys_bytes, h * BANK * 4, (h + 1) * BANK * 4, "keys_w%d" % h) for h in range(2)]
+        keys_w = [load_words(keys_bytes, 0, BANK * 4, "keys_w0")]
         l1 = load_list(offs, "l1")
-        load_plane(keys_plane, keys_scales)
+        keys_w.append(load_words(keys_bytes, BANK * 4, POOL * 4, "keys_w1"))
         l2 = load_list(offs2, "l2")
         users_w = load_words(users_words[0].rearrange("p n t -> p (n t)"), 0, POOL * 4, "users_w")
         load_plane(users_plane, users_scales)
@@ -86,12 +89,17 @@ def tile_attend_estuary_four_kernel(tc, query, keys_words, keys_scales, notes_wo
         load_plane(shelves_plane, shelves_scales)
         l6 = load_list(offs6, "l6")
 
-        q_bf = sb.tile([P, Q, PACK], BF16, name="q_bf", align_bytes=64)
-        nc.vector.tensor_copy(q_bf[:], q_raw[:].rearrange("p j q -> p q j"))
+        q_bf = sb.tile([P, Q, PACK], BF16, name="q_bf", tag="q_bf_then_f2", align_bytes=64)
+        q_by_row = q_raw[:].rearrange("p j q -> p q j")
+        nc.scalar.copy(q_bf[:, 0:Q_SCALAR, :], q_by_row[:, 0:Q_SCALAR, :])
+        nc.vector.tensor_copy(q_bf[:, Q_SCALAR:Q, :], q_by_row[:, Q_SCALAR:Q, :])
         q_codes = sb.tile([P, Q], U32, name="q_codes", align_bytes=64)
         q_plane = sb.tile([P, Q], U8, name="q_plane", align_bytes=64)
         nc.vector.quantize_mx(out=q_codes[:].bitcast(FP8X4), scales=q_plane[:],
                               in_=q_bf[:].rearrange("p q j -> p (q j)"))
+
+        f2 = sb.tile([P, POOL], F32, name="f2", tag="q_bf_then_f2", align_bytes=64)
+        nc.vector.memset(f2[:], 0.0)
 
         def scores(words, plane, width, tag):
             bank = ps.tile([P, width], F32, name=tag, tag=tag)
@@ -110,10 +118,14 @@ def tile_attend_estuary_four_kernel(tc, query, keys_words, keys_scales, notes_wo
             else:
                 nc.vector.tensor_copy(a_sb[:, cols], bank[:])
 
-        for h in range(2):
-            ga = sb.tile([P, HALF], F32, name="ga%d" % h)
-            nc.scalar.activation(ga[:], a_sb[:].indirect(half_of(l1, h)), COPY)
-            nc.vector.tensor_copy(f1[:].indirect(half_of(l2, h)), ga[:])
+        def gather(window, offsets, name):
+            picked = sb.tile([P, SLOTS], F32, name=name)
+            nc.scalar.activation(picked[:, 0:HALF], window[:].indirect(half_of(offsets, 0)), COPY)
+            nc.vector.tensor_copy(picked[:, HALF:SLOTS], window[:].indirect(half_of(offsets, 1)))
+            return picked
+
+        ga = gather(a_sb, l1, "ga")
+        nc.vector.tensor_copy(f1[:].indirect(l2[:]), ga[:])
 
         c_sb = sb.tile([P, POOL], F32, name="c_sb")
         for h in range(2):
@@ -130,14 +142,10 @@ def tile_attend_estuary_four_kernel(tc, query, keys_words, keys_scales, notes_wo
                           notes_plane[:, cols], BANK, "bank_b%d" % h)
             nc.vector.tensor_tensor(bb[:, cols], bank[:], f1[:, cols], ADD)
 
-        gb = [sb.tile([P, HALF], F32, name="gb%d" % h) for h in range(2)]
-        nc.scalar.activation(gb[0][:], bb[:].indirect(half_of(l3, 0)), COPY)
-        nc.vector.tensor_copy(gb[1][:], bb[:].indirect(half_of(l3, 1)))
-        w = [sb.tile([P, HALF], F32, name="w%d" % h) for h in range(2)]
-        for h in range(2):
-            nc.vector.tensor_tensor(w[h][:], gb[h][:], cg[:, h * HALF:(h + 1) * HALF], MAX)
-        for h in range(2):
-            nc.vector.tensor_copy(f2[:].indirect(half_of(l5, h)), w[h][:])
+        gb = gather(bb, l3, "gb")
+        w = sb.tile([P, SLOTS], F32, name="w")
+        nc.vector.tensor_tensor(w[:], gb[:], cg[:], MAX)
+        nc.vector.tensor_copy(f2[:].indirect(l5[:]), w[:])
 
         dd = sb.tile([P, POOL], F32, name="dd")
         for h in range(2):

@@ -25,8 +25,9 @@ SLOTS = 512
 HALF = SLOTS // 2
 LIST_COLS = SLOTS // 16
 BANK = 512
-QUARTER = 256
 Q_SCALAR = 40
+A_WIDTHS = (256, 256, 256, 128, 128)
+TAIL = 320
 
 
 def tile_attend_estuary_four_kernel(tc, query, keys_words, keys_scales, notes_words, notes_scales,
@@ -108,15 +109,16 @@ def tile_attend_estuary_four_kernel(tc, query, keys_words, keys_scales, notes_wo
             return bank
 
         a_sb = sb.tile([P, POOL], F32, name="a_sb")
-        for j in range(POOL // QUARTER):
-            h, r = divmod(j, 2)
-            bank = scores(keys_w[h][:, r * QUARTER * 4:(r + 1) * QUARTER * 4].bitcast(FP8X4),
-                          keys_plane[:, j * QUARTER:(j + 1) * QUARTER], QUARTER, "bank_a%d" % j)
-            cols = slice(j * QUARTER, (j + 1) * QUARTER)
+        start = 0
+        for j, width in enumerate(A_WIDTHS):
+            h, r = divmod(start, BANK)
+            cols = slice(start, start + width)
+            bank = scores(keys_w[h][:, r * 4:(r + width) * 4].bitcast(FP8X4), keys_plane[:, cols], width, "bank%d" % j)
             if j % 2 == 0:
                 nc.scalar.copy(a_sb[:, cols], bank[:])
             else:
                 nc.vector.tensor_copy(a_sb[:, cols], bank[:])
+            start = start + width
 
         def gather(window, offsets, name):
             picked = sb.tile([P, SLOTS], F32, name=name)
@@ -130,29 +132,36 @@ def tile_attend_estuary_four_kernel(tc, query, keys_words, keys_scales, notes_wo
         c_sb = sb.tile([P, POOL], F32, name="c_sb")
         for h in range(2):
             bank = scores(users_w[:, h * BANK * 4:(h + 1) * BANK * 4].bitcast(FP8X4),
-                          users_plane[:, h * BANK:(h + 1) * BANK], BANK, "bank_a%d" % (2 + h))
+                          users_plane[:, h * BANK:(h + 1) * BANK], BANK, "bank%d" % (3 + h))
             nc.scalar.copy(c_sb[:, h * BANK:(h + 1) * BANK], bank[:])
         cg = sb.tile([P, SLOTS], F32, name="cg")
         nc.scalar.activation(cg[:], c_sb[:].indirect(l4[:]), COPY)
 
-        bb = sb.tile([P, POOL], F32, name="bb")
-        for h in range(2):
-            cols = slice(h * BANK, (h + 1) * BANK)
-            bank = scores(notes_w[:, h * BANK * 2:(h + 1) * BANK * 2].bitcast(FP4X4),
-                          notes_plane[:, cols], BANK, "bank_b%d" % h)
-            nc.vector.tensor_tensor(bb[:, cols], bank[:], f1[:, cols], ADD)
+        def fp4_scores(words, plane, first_bank, name):
+            banks = [scores(words[:, h * BANK * 2:(h + 1) * BANK * 2].bitcast(FP4X4),
+                            plane[:, h * BANK:(h + 1) * BANK], BANK, "bank%d" % (first_bank + h)) for h in range(2)]
+            tail = sb.tile([P, TAIL], F32, name=name)
+            nc.scalar.copy(tail[:], banks[1][:, BANK - TAIL:BANK])
+            return banks, tail
+
+        def combine(banks, tail, placed, op, name):
+            whole = sb.tile([P, POOL], F32, name=name)
+            nc.gpsimd.tensor_tensor(whole[:, POOL - TAIL:POOL], tail[:], placed[:, POOL - TAIL:POOL], op)
+            nc.vector.tensor_tensor(whole[:, 0:BANK], banks[0][:], placed[:, 0:BANK], op)
+            nc.vector.tensor_tensor(whole[:, BANK:POOL - TAIL], banks[1][:, 0:BANK - TAIL],
+                                    placed[:, BANK:POOL - TAIL], op)
+            return whole
+
+        b_banks, b_tail = fp4_scores(notes_w, notes_plane, 5, "b_tail")
+        d_banks, d_tail = fp4_scores(shelves_w, shelves_plane, 0, "d_tail")
+        bb = combine(b_banks, b_tail, f1, ADD, "bb")
 
         gb = gather(bb, l3, "gb")
         w = sb.tile([P, SLOTS], F32, name="w")
         nc.vector.tensor_tensor(w[:], gb[:], cg[:], MAX)
         nc.vector.tensor_copy(f2[:].indirect(l5[:]), w[:])
 
-        dd = sb.tile([P, POOL], F32, name="dd")
-        for h in range(2):
-            cols = slice(h * BANK, (h + 1) * BANK)
-            bank = scores(shelves_w[:, h * BANK * 2:(h + 1) * BANK * 2].bitcast(FP4X4),
-                          shelves_plane[:, cols], BANK, "bank_d%d" % h)
-            nc.vector.tensor_tensor(dd[:, cols], bank[:], f2[:, cols], SUB)
+        dd = combine(d_banks, d_tail, f2, SUB, "dd")
 
         y0 = sb.tile([P, HALF], F32, name="y0")
         nc.vector.tensor_tensor(y0[:], dd[:].indirect(half_of(l6, 0)), cg[:, 0:HALF], ADD)

@@ -61,7 +61,7 @@ def tile_attend_estuary_four_kernel(tc, query, keys_words, keys_scales, notes_wo
             nc.sync.dma_start(tile[:].bitcast(I32), src[:, c0:c1].bitcast(I32))
             return tile
 
-        keys_plane = sb.tile([P, POOL], U8, name="keys_plane", align_bytes=64)
+        keys_plane = zeroed_plane("keys_plane", nc.gpsimd)
         f1 = sb.tile([P, POOL], F32, name="f1")
         nc.vector.memset(f1[:], 0.0)
         users_plane = zeroed_plane("users_plane", nc.vector)
@@ -70,14 +70,10 @@ def tile_attend_estuary_four_kernel(tc, query, keys_words, keys_scales, notes_wo
 
         q_raw = sb.tile([P, PACK, Q], F32, name="q_raw")
         nc.sync.dma_start(q_raw[:], query.rearrange("(p j) q -> p j q", j=PACK))
-        key_rows = keys_scales[0].bitcast(I32)
-        for quad in range(4):
-            nc.sync.dma_start(keys_plane[32 * quad:32 * quad + 32, :].bitcast(I32),
-                              key_rows[4 * quad:4 * quad + 4, :].unsqueeze(0).to_broadcast([8, 4, POOL // 4]))
+        load_plane(keys_plane, keys_scales)
         keys_bytes = keys_words[0].rearrange("p n t -> p (n t)")
-        keys_w = [load_words(keys_bytes, 0, BANK * 4, "keys_w0")]
+        keys_w = [load_words(keys_bytes, h * BANK * 4, (h + 1) * BANK * 4, "keys_w%d" % h) for h in range(2)]
         l1 = load_list(offs, "l1")
-        keys_w.append(load_words(keys_bytes, BANK * 4, POOL * 4, "keys_w1"))
         l2 = load_list(offs2, "l2")
         users_w = load_words(users_words[0].rearrange("p n t -> p (n t)"), 0, POOL * 4, "users_w")
         load_plane(users_plane, users_scales)

from contextlib import ExitStack

import concourse.mybir as mybir

FLOPS = 536870912

F32 = mybir.dt.float32
BF16 = mybir.dt.bfloat16
I32 = mybir.dt.int32
U32 = mybir.dt.uint32
U16 = mybir.dt.uint16
U8 = mybir.dt.uint8
FP8X4 = mybir.dt.float8_e4m3fn_x4
FP4X4 = mybir.dt.float4_e2m1fn_x4
ADD = mybir.AluOpType.add
SUB = mybir.AluOpType.subtract
MAX = mybir.AluOpType.max
COPY = mybir.ActivationFunctionType.Copy

P = 128
PACK = 4
Q = 128
POOL = 1024
SLOTS = 512
HALF = SLOTS // 2
LIST_COLS = SLOTS // 16
BANK = 512
Q_SCALAR = 40
A_WIDTHS = (256, 256, 256, 128, 128)
TAIL = 320


def tile_attend_estuary_four_kernel(tc, query, keys_words, keys_scales, notes_words, notes_scales,
                                     users_words, users_scales, shelves_words, shelves_scales,
                                     offs, offs2, offs3, offs4, offs5, offs6, out):
    nc = tc.nc
    with ExitStack() as ctx:
        sb = ctx.enter_context(tc.tile_pool(name="sb", bufs=1))
        ps = ctx.enter_context(tc.psum_pool(name="ps", bufs=1))

        def load_list(src, name):
            tile = sb.tile([P, LIST_COLS], U16, name=name)
            nc.sync.dma_start(tile[:], src)
            return tile

        def half_of(offsets, h):
            return offsets[:, h * (LIST_COLS // 2):(h + 1) * (LIST_COLS // 2)]

        def zeroed_plane(name, engine):
            plane = sb.tile([P, POOL], U8, name=name, align_bytes=64)
            engine.memset(plane[:].bitcast(I32), 0)
            return plane

        def load_plane(plane, src):
            rows = src[0].bitcast(I32)
            for quad in range(4):
                nc.sync.dma_start(plane[32 * quad:32 * quad + 4, :].bitcast(I32), rows[4 * quad:4 * quad + 4, :])

        def load_words(src, c0, c1, name):
            tile = sb.tile([P, c1 - c0], U8, name=name, align_bytes=64)
            nc.sync.dma_start(tile[:].bitcast(I32), src[:, c0:c1].bitcast(I32))
            return tile

        keys_plane = zeroed_plane("keys_plane", nc.gpsimd)
        f1 = sb.tile([P, POOL], F32, name="f1")
        nc.vector.memset(f1[:], 0.0)
        users_plane = zeroed_plane("users_plane", nc.vector)
        notes_plane = zeroed_plane("notes_plane", nc.vector)
        shelves_plane = zeroed_plane("shelves_plane", nc.vector)

        q_raw = sb.tile([P, PACK, Q], F32, name="q_raw")
        nc.sync.dma_start(q_raw[:], query.rearrange("(p j) q -> p j q", j=PACK))
        load_plane(keys_plane, keys_scales)
        keys_bytes = keys_words[0].rearrange("p n t -> p (n t)")
        keys_w = [load_words(keys_bytes, h * BANK * 4, (h + 1) * BANK * 4, "keys_w%d" % h) for h in range(2)]
        l1 = load_list(offs, "l1")
        l2 = load_list(offs2, "l2")
        users_w = load_words(users_words[0].rearrange("p n t -> p (n t)"), 0, POOL * 4, "users_w")
        load_plane(users_plane, users_scales)
        l4 = load_list(offs4, "l4")
        notes_w = load_words(notes_words[0], 0, POOL * 2, "notes_w")
        load_plane(notes_plane, notes_scales)
        l3 = load_list(offs3, "l3")
        l5 = load_list(offs5, "l5")
        shelves_w = load_words(shelves_words[0], 0, POOL * 2, "shelves_w")
        load_plane(shelves_plane, shelves_scales)
        l6 = load_list(offs6, "l6")

        q_bf = sb.tile([P, Q, PACK], BF16, name="q_bf", tag="q_bf_then_f2", align_bytes=64)
        q_by_row = q_raw[:].rearrange("p j q -> p q j")
        nc.scalar.copy(q_bf[:, 0:Q_SCALAR, :], q_by_row[:, 0:Q_SCALAR, :])
        nc.vector.tensor_copy(q_bf[:, Q_SCALAR:Q, :], q_by_row[:, Q_SCALAR:Q, :])
        q_codes = sb.tile([P, Q], U32, name="q_codes", align_bytes=64)
        q_plane = sb.tile([P, Q], U8, name="q_plane", align_bytes=64)
        nc.vector.quantize_mx(out=q_codes[:].bitcast(FP8X4), scales=q_plane[:],
                              in_=q_bf[:].rearrange("p q j -> p (q j)"))

        f2 = sb.tile([P, POOL], F32, name="f2", tag="q_bf_then_f2", align_bytes=64)
        nc.vector.memset(f2[:], 0.0)

        def scores(words, plane, width, tag):
            bank = ps.tile([P, width], F32, name=tag, tag=tag)
            nc.tensor.matmul_mx(out=bank[:], lhsT=q_codes[:].bitcast(FP8X4), lhsT_scale=q_plane[:],
                                rhs=words, rhs_scale=plane, start=True, stop=True)
            return bank

        a_sb = sb.tile([P, POOL], F32, name="a_sb")
        start = 0
        for j, width in enumerate(A_WIDTHS):
            h, r = divmod(start, BANK)
            cols = slice(start, start + width)
            bank = scores(keys_w[h][:, r * 4:(r + width) * 4].bitcast(FP8X4), keys_plane[:, cols], width, "bank%d" % j)
            if j % 2 == 0:
                nc.scalar.copy(a_sb[:, cols], bank[:])
            else:
                nc.vector.tensor_copy(a_sb[:, cols], bank[:])
            start = start + width

        def gather(window, offsets, name):
            picked = sb.tile([P, SLOTS], F32, name=name)
            nc.scalar.activation(picked[:, 0:HALF], window[:].indirect(half_of(offsets, 0)), COPY)
            nc.vector.tensor_copy(picked[:, HALF:SLOTS], window[:].indirect(half_of(offsets, 1)))
            return picked

        ga = gather(a_sb, l1, "ga")
        nc.vector.tensor_copy(f1[:].indirect(l2[:]), ga[:])

        c_sb = sb.tile([P, POOL], F32, name="c_sb")
        for h in range(2):
            bank = scores(users_w[:, h * BANK * 4:(h + 1) * BANK * 4].bitcast(FP8X4),
                          users_plane[:, h * BANK:(h + 1) * BANK], BANK, "bank%d" % (3 + h))
            nc.scalar.copy(c_sb[:, h * BANK:(h + 1) * BANK], bank[:])
        cg = sb.tile([P, SLOTS], F32, name="cg")
        nc.scalar.activation(cg[:], c_sb[:].indirect(l4[:]), COPY)

        def fp4_scores(words, plane, first_bank, name):
            banks = [scores(words[:, h * BANK * 2:(h + 1) * BANK * 2].bitcast(FP4X4),
                            plane[:, h * BANK:(h + 1) * BANK], BANK, "bank%d" % (first_bank + h)) for h in range(2)]
            tail = sb.tile([P, TAIL], F32, name=name)
            nc.scalar.copy(tail[:], banks[1][:, BANK - TAIL:BANK])
            return banks, tail

        def combine(banks, tail, placed, op, name):
            whole = sb.tile([P, POOL], F32, name=name)
            nc.gpsimd.tensor_tensor(whole[:, POOL - TAIL:POOL], tail[:], placed[:, POOL - TAIL:POOL], op)
            nc.vector.tensor_tensor(whole[:, 0:BANK], banks[0][:], placed[:, 0:BANK], op)
            nc.vector.tensor_tensor(whole[:, BANK:POOL - TAIL], banks[1][:, 0:BANK - TAIL],
                                    placed[:, BANK:POOL - TAIL], op)
            return whole

        b_banks, b_tail = fp4_scores(notes_w, notes_plane, 5, "b_tail")
        d_banks, d_tail = fp4_scores(shelves_w, shelves_plane, 0, "d_tail")
        bb = combine(b_banks, b_tail, f1, ADD, "bb")

        gb = gather(bb, l3, "gb")
        w = sb.tile([P, SLOTS], F32, name="w")
        nc.vector.tensor_tensor(w[:], gb[:], cg[:], MAX)
        nc.vector.tensor_copy(f2[:].indirect(l5[:]), w[:])

        dd = combine(d_banks, d_tail, f2, SUB, "dd")

        y0 = sb.tile([P, HALF], F32, name="y0")
        nc.vector.tensor_tensor(y0[:], dd[:].indirect(half_of(l6, 0)), cg[:, 0:HALF], ADD)
        nc.sync.dma_start(out[:, 0:HALF], y0[:])
        gd = sb.tile([P, HALF], F32, name="gd")
        nc.scalar.activation(gd[:], dd[:].indirect(half_of(l6, 1)), COPY)
        y1 = sb.tile([P, HALF], F32, name="y1")
        nc.vector.tensor_tensor(y1[:], gd[:], cg[:, HALF:SLOTS], ADD)
        nc.sync.dma_start(out[:, HALF:SLOTS], y1[:])
